import numpy as np
import ml_dtypes


def mxq(x, axis, fmt="e4m3"):
    dtype, down = {"e4m3": (ml_dtypes.float8_e4m3fn, 7), "e5m2": (ml_dtypes.float8_e5m2, 14)}[fmt]
    v = np.moveaxis(np.asarray(x, np.float32).astype(ml_dtypes.bfloat16).astype(np.float64), axis, -1)
    blocks = v.reshape(v.shape[:-1] + (-1, 32))
    amax = np.abs(blocks).max(-1, keepdims=True)
    byte = np.maximum(np.where(amax > 0, np.frexp(amax)[1] - 1 + 127, 0) - down, 1)
    scale = np.exp2(byte - 127.0)
    codes = (blocks / scale).astype(np.float32).astype(dtype).astype(np.float64)
    return np.moveaxis((codes * scale).reshape(v.shape), -1, axis)


WIDE = False


def mx_kscale(k):
    if not WIDE:
        return np.ones(k)
    levels = np.array([10, -10, 5, -5, 0])
    if k % 512:
        return np.exp2(np.random.permutation(np.resize(levels, k // 32))).repeat(32)
    a = np.empty((k // 512, 16))
    for p in range(k // 512):
        a[p, :8] = np.random.permutation(np.resize(levels, 8))
        for g in range(8):
            far = levels[np.abs(levels - a[p, g]) >= 10]
            a[p, g + 8] = far[np.random.randint(len(far))]
    return np.exp2(a.ravel()).repeat(32)


def f64(x):
    return np.asarray(x).astype(np.float64)


def striped(idx):
    return np.tile(idx.reshape(-1, 16).T, (8, 1)).astype(np.uint16)


def unstriped(offs):
    return offs[:16].T.reshape(-1).astype(np.int64)


def pack_weight(w):
    k, n = w.shape
    w = f64(np.asarray(w, np.float32).astype(ml_dtypes.bfloat16)).reshape(k // 32, 32, n)
    amax = np.abs(w).max(1)
    byte = np.clip(np.where(amax > 0, np.frexp(amax)[1] - 1 + 127 - 7, 1), 1, 254)
    scaled = (w * np.exp2(127.0 - byte)[:, None, :]).reshape(k, n).astype(np.float32)
    words = np.ascontiguousarray(scaled.reshape(k // 512, 128, 4, n).transpose(0, 1, 3, 2)).astype(ml_dtypes.float8_e4m3fn).view(np.uint8)
    return words, np.ascontiguousarray(byte.astype(np.uint8).reshape(k // 512, 16, n))


def unpack_weight(words, scales):
    g, p, n, _ = words.shape
    vals = np.ascontiguousarray(words).view(ml_dtypes.float8_e4m3fn).astype(np.float64) * np.repeat(np.exp2(scales.astype(np.float64) - 127.0), 8, axis=1)[..., None]
    return vals.transpose(0, 1, 3, 2).reshape(g * 512, n)


def planes(y):
    n, m = y.shape
    v = y.astype(np.float32).astype(ml_dtypes.bfloat16).astype(np.float64).reshape(n // 32, 32, m)
    top = np.abs(v).max(1)
    byte = np.clip(np.where(top > 0, np.frexp(top)[1] - 1 + 127 - 7, 1), 1, 254)
    codes = (v * np.exp2(127.0 - byte)[:, None, :]).reshape(n, m).astype(np.float32).astype(ml_dtypes.float8_e4m3fn).view(np.uint8)
    words = codes.reshape(n // 512, 128, 4, m).transpose(0, 1, 3, 2)
    return np.ascontiguousarray(words), np.ascontiguousarray(byte.astype(np.uint8).reshape(n // 512, 16, m))


K, T, S, D, H, N, V = 512, 2048, 512, 8, 512, 512, 64


def setup_inputs():
    n = np.random.standard_normal
    s = mx_kscale(K)[:, None]
    u = mx_kscale(H)
    packed_xT = pack_weight(n((K, T)) * s)
    return {
        "x_words": packed_xT[0],
        "x_scales": packed_xT[1],
        "w1": (n((K, H)) / np.sqrt(K) / s * u).astype(np.float32),
        "obs": (n((H, V)) * u[:, None]).astype(np.float32),
        "w2": (n((H, N)) / np.sqrt(H) / u[:, None]).astype(np.float32),
        "ens": (n((N, T))).astype(np.float32),
        "offs": striped(np.random.permutation(T)[:S]),
    }


def reference(x_words, x_scales, w1, obs, w2, ens, offs):
    xq = unpack_weight(x_words, x_scales)[:, unstriped(offs)]
    y = mxq(f64(w1), 0, "e4m3").T @ xq
    my = y.reshape(len(y), -1, D).mean(axis=2)
    om = f64(obs) - (0.5 * my)
    rr = np.repeat(om, D, axis=1) - (0.5 * y)
    out_0 = f64(ens)[:, unstriped(offs)] + (mxq(f64(w2), 0, "e4m3").T @ mxq(rr, 0, "e4m3"))
    return (out_0,) + planes(out_0)

@@ -1,0 +1,226 @@
+from contextlib import ExitStack
+
+import concourse.mybir as mybir
+
+K, T, S, D, H, N, V = 512, 2048, 512, 8, 512, 512, 64
+FLOPS = 2 * K * H * S + 2 * H * N * S
+
+F32 = mybir.dt.float32
+BF16 = mybir.dt.bfloat16
+I32 = mybir.dt.int32
+U32 = mybir.dt.uint32
+U16 = mybir.dt.uint16
+U8 = mybir.dt.uint8
+FP8X4 = mybir.dt.float8_e4m3fn_x4
+ALU = mybir.AluOpType
+
+P = 128
+PACK = 4
+LANES = 16
+BLOCK = 128
+HALF = 256
+
+
+def tile_picked_yenkf_half_po_kernel(tc, x_words, x_scales, w1, obs, w2, ens, offs, out_0, out_1, out_2):
+    nc = tc.nc
+    with ExitStack() as ctx:
+        keep = ctx.enter_context(tc.tile_pool(name="keep", bufs=1))
+        psum = ctx.enter_context(tc.psum_pool(name="psum", bufs=1))
+
+        offsets = keep.tile([P, S // LANES], U16, name="offsets")
+        nc.sync.dma_start(offsets[:], offs)
+
+        x_scale_table = keep.tile([P, T], U8, name="x_scale_table", align_bytes=64)
+        nc.vector.memset(x_scale_table[:].bitcast(I32), 0)
+        w1_rows = w1.rearrange("(p j) c -> p j c", j=PACK)
+        w1_raw = [keep.tile([P, 2, H], F32, name=f"w1_raw{u}") for u in range(2)]
+        nc.sync.dma_start(out=w1_raw[0][:], in_=w1_rows[:, 0:2, :])
+        for q in range(4):
+            nc.sync.dma_start(
+                out=x_scale_table[32 * q : 32 * q + 4, :].bitcast(I32),
+                in_=x_scales[0, 4 * q : 4 * q + 4, :].bitcast(I32),
+            )
+        nc.sync.dma_start(out=w1_raw[1][:], in_=w1_rows[:, 2:4, :])
+        x_word_table = keep.tile([P, T], I32, name="x_word_table", align_bytes=64)
+        nc.sync.dma_start(out=x_word_table[:], in_=x_words[0].rearrange("p n t -> p (n t)").bitcast(I32))
+        obs_sb = keep.tile([P, PACK, V], F32, name="obs_sb")
+        nc.sync.dma_start(out=obs_sb[:], in_=obs.rearrange("(p t) v -> p t v", t=PACK))
+        w2_raw = keep.tile([P, PACK, N], F32, name="w2_raw")
+        nc.sync.dma_start(out=w2_raw[:], in_=w2.rearrange("(p j) c -> p j c", j=PACK))
+        ens_rows = ens.rearrange("(p t) c -> p t c", t=PACK)
+        ens_table = []
+        for t in range(PACK):
+            table = keep.tile([P, T], F32, name=f"ens_table{t}")
+            nc.sync.dma_start(out=table[:], in_=ens_rows[:, t, :])
+            ens_table.append(table)
+
+        def half_list(h):
+            return offsets[:, h * (HALF // LANES) : (h + 1) * (HALF // LANES)]
+
+        w1_bf = keep.tile([P, H * PACK], BF16, name="w1_bf", align_bytes=64)
+
+        def round_w1(u):
+            nc.vector.tensor_scalar(
+                out=w1_bf[:].rearrange("p (t m j) -> p m j t", t=PACK, j=PACK)[:, :, 2 * u : 2 * u + 2, :],
+                in0=w1_raw[u][:].rearrange("p j (m t) -> p m j t", t=PACK),
+                scalar1=0.5,
+                scalar2=None,
+                op0=ALU.mult,
+            )
+
+        round_w1(0)
+        x_scale = keep.tile([P, S], U8, name="x_scale", align_bytes=64)
+        nc.vector.tensor_copy(x_scale[:], x_scale_table[:].indirect(offsets[:]))
+        round_w1(1)
+        w1_codes = keep.tile([P, H], U32, name="w1_codes", align_bytes=64)
+        w1_scale = keep.tile([P, H], U8, name="w1_scale", align_bytes=64)
+        nc.vector.quantize_mx(out=w1_codes[:].bitcast(FP8X4), scales=w1_scale[:], in_=w1_bf[:])
+
+        w2_bf = keep.tile([P, N * PACK], BF16, name="w2_bf", tag="bf_stage", align_bytes=64)
+        nc.scalar.copy(
+            out=w2_bf[:].rearrange("p (t m j) -> p m j t", t=PACK, j=PACK),
+            in_=w2_raw[:].rearrange("p j (m t) -> p m j t", t=PACK),
+        )
+        w2_codes = keep.tile([P, N], U32, name="w2_codes", align_bytes=64)
+        w2_scale = keep.tile([P, N], U8, name="w2_scale", align_bytes=64)
+
+        x_codes = []
+        for h in range(2):
+            picked = keep.tile([P, HALF], U32, name=f"x_codes{h}", align_bytes=64)
+            nc.vector.tensor_copy(picked[:], x_word_table[:].bitcast(U32).indirect(half_list(h)))
+            x_codes.append(picked)
+
+        y_bank = []
+        for b in range(S // BLOCK):
+            bank = psum.tile([P, PACK, BLOCK], F32, name=f"y_bank{b}")
+            cols = slice((b % 2) * BLOCK, (b % 2 + 1) * BLOCK)
+            for t in range(PACK):
+                nc.tensor.matmul_mx(
+                    out=bank[:, t, :],
+                    lhsT=w1_codes[:, t * P : (t + 1) * P].bitcast(FP8X4),
+                    lhsT_scale=w1_scale[:, t * P : (t + 1) * P],
+                    rhs=x_codes[b // 2][:, cols].bitcast(FP8X4),
+                    rhs_scale=x_scale[:, b * BLOCK : (b + 1) * BLOCK],
+                    start=True,
+                    stop=True,
+                )
+            y_bank.append(bank)
+
+        groups = BLOCK // D
+        sums = [keep.tile([P, groups, PACK], F32, name=f"sums{b}") for b in range(4)]
+        om = [keep.tile([P, groups, PACK], F32, name=f"om{b}") for b in range(4)]
+        rr_bf = [keep.tile([P, HALF * PACK], BF16, name="rr_bf0", align_bytes=64)]
+        rr_codes = [keep.tile([P, HALF], U32, name=f"rr_codes{h}", align_bytes=64) for h in range(2)]
+        rr_scale = [keep.tile([P, HALF], U8, name=f"rr_scale{h}", align_bytes=64) for h in range(2)]
+        update = [keep.tile([P, 2, S], F32, name=f"update{u}") for u in range(2)]
+        result = [keep.tile([P, 2, S], F32, name=f"result{u}") for u in range(2)]
+
+        def member_sums(b):
+            nc.vector.tensor_reduce(
+                out=sums[b][:],
+                in_=y_bank[b][:].rearrange("p t (v d) -> p v t d", d=D),
+                axis=mybir.AxisListType.X,
+                op=ALU.add,
+            )
+
+        def innovation(b):
+            nc.vector.scalar_tensor_tensor(
+                out=om[b][:],
+                in0=sums[b][:],
+                scalar=-1.0 / D,
+                in1=obs_sb[:, :, b * groups : (b + 1) * groups].rearrange("p t v -> p v t"),
+                op0=ALU.mult,
+                op1=ALU.add,
+            )
+
+        def residual(b):
+            span = slice((b % 2) * BLOCK * PACK, (b % 2 + 1) * BLOCK * PACK)
+            nc.vector.tensor_tensor(
+                out=rr_bf[b // 2][:, span].rearrange("p (v d t) -> p v d t", d=D, t=PACK),
+                in0=om[b][:].unsqueeze(2).broadcast_to([P, groups, D, PACK]),
+                in1=y_bank[b][:].rearrange("p t (v d) -> p v d t", d=D),
+                op=ALU.subtract,
+            )
+
+        def second_product(h):
+            nc.vector.quantize_mx(out=rr_codes[h][:].bitcast(FP8X4), scales=rr_scale[h][:], in_=rr_bf[h][:])
+            for u in range(2):
+                bank = psum.tile([P, 2, HALF], F32, name=f"z_bank{h}{u}")
+                for e in range(2):
+                    t = 2 * u + e
+                    nc.tensor.matmul_mx(
+                        out=bank[:, e, :],
+                        lhsT=w2_codes[:, t * P : (t + 1) * P].bitcast(FP8X4),
+                        lhsT_scale=w2_scale[:, t * P : (t + 1) * P],
+                        rhs=rr_codes[h][:].bitcast(FP8X4),
+                        rhs_scale=rr_scale[h][:],
+                        start=True,
+                        stop=True,
+                    )
+                nc.scalar.copy(out=update[u][:, :, h * HALF : (h + 1) * HALF], in_=bank[:])
+
+        member_sums(0)
+        member_sums(1)
+        innovation(0)
+        member_sums(2)
+        innovation(1)
+        residual(0)
+        member_sums(3)
+        residual(1)
+        innovation(2)
+        nc.vector.quantize_mx(out=w2_codes[:].bitcast(FP8X4), scales=w2_scale[:], in_=w2_bf[:])
+        rr_bf.append(keep.tile([P, HALF * PACK], BF16, name="rr_bf1", tag="bf_stage", align_bytes=64))
+        innovation(3)
+        second_product(0)
+        residual(2)
+        residual(3)
+        second_product(1)
+
+        out_rows = out_0.rearrange("(p t) c -> p t c", t=PACK)
+        out_bf = [keep.tile([P, HALF, PACK], BF16, name=f"out_bf{h}", align_bytes=64) for h in range(2)]
+        out_codes = keep.tile([P, S], U32, name="out_codes", align_bytes=64)
+        out_scale = keep.tile([P, S], U8, name="out_scale", align_bytes=64)
+        out_words = out_1[0].rearrange("p n t -> p (n t)").bitcast(I32)
+
+        def add_states(t, h):
+            cols = slice(h * HALF, (h + 1) * HALF)
+            nc.vector.tensor_tensor(
+                result[t // 2][:, t % 2, cols],
+                ens_table[t][:].indirect(half_list(h)),
+                update[t // 2][:, t % 2, cols],
+                ALU.add,
+            )
+
+        def round_pair(copy, u, h):
+            cols = slice(h * HALF, (h + 1) * HALF)
+            copy(out=out_bf[h][:, :, 2 * u : 2 * u + 2], in_=result[u][:, :, cols].rearrange("p e c -> p c e"))
+
+        def quantise_result(h):
+            cols = slice(h * HALF, (h + 1) * HALF)
+            nc.vector.quantize_mx(
+                out=out_codes[:, cols].bitcast(FP8X4),
+                scales=out_scale[:, cols],
+                in_=out_bf[h][:].rearrange("p c t -> p (c t)"),
+            )
+            nc.sync.dma_start(out=out_words[:, cols], in_=out_codes[:, cols].bitcast(I32))
+
+        for h in range(2):
+            add_states(0, h)
+            add_states(1, h)
+            round_pair(nc.scalar.copy, 0, h)
+        nc.sync.dma_start(out=out_rows[:, 0:2, :], in_=result[0][:])
+        nc.vector.tensor_tensor(result[1][:, 0, :], ens_table[2][:].indirect(offsets[:]), update[1][:, 0, :], ALU.add)
+        nc.sync.dma_start(out=out_rows[:, 2, :], in_=result[1][:, 0, :])
+        add_states(3, 0)
+        round_pair(nc.scalar.copy, 1, 0)
+        add_states(3, 1)
+        nc.sync.dma_start(out=out_rows[:, 3, :], in_=result[1][:, 1, :])
+        round_pair(nc.vector.tensor_copy, 1, 1)
+        quantise_result(0)
+        quantise_result(1)
+        for q in range(4):
+            queue = nc.scalar if q % 2 == 0 else nc.sync
+            queue.dma_start(
+                out=out_2[0, 4 * q : 4 * q + 4, :].bitcast(I32),
+                in_=out_scale[32 * q : 32 * q + 4, :].bitcast(I32),
+            )

@@ -31,16 +31,17 @@ def tile_picked_yenkf_half_po_kernel(tc, x_words, x_scales, w1, obs, w2, ens, of
         nc.sync.dma_start(offsets[:], offs)
 
         x_scale_table = keep.tile([P, T], U8, name="x_scale_table", align_bytes=64)
-        nc.vector.memset(x_scale_table[:].bitcast(I32), 0)
-        w1_rows = w1.rearrange("(p j) c -> p j c", j=PACK)
-        w1_raw = [keep.tile([P, 2, H], F32, name=f"w1_raw{u}") for u in range(2)]
-        nc.sync.dma_start(out=w1_raw[0][:], in_=w1_rows[:, 0:2, :])
+        nc.vector.memset(x_scale_table[:, : T // 2].bitcast(I32), 0)
+        nc.gpsimd.memset(x_scale_table[:, T // 2 :].bitcast(I32), 0)
         for q in range(4):
             nc.sync.dma_start(
                 out=x_scale_table[32 * q : 32 * q + 4, :].bitcast(I32),
                 in_=x_scales[0, 4 * q : 4 * q + 4, :].bitcast(I32),
             )
-        nc.sync.dma_start(out=w1_raw[1][:], in_=w1_rows[:, 2:4, :])
+        w1_rows = w1.rearrange("(p j) c -> p j c", j=PACK)
+        w1_raw = [keep.tile([P, 2, H], F32, name=f"w1_raw{u}") for u in range(2)]
+        for u in range(2):
+            nc.sync.dma_start(out=w1_raw[u][:], in_=w1_rows[:, 2 * u : 2 * u + 2, :])
         x_word_table = keep.tile([P, T], I32, name="x_word_table", align_bytes=64)
         nc.sync.dma_start(out=x_word_table[:], in_=x_words[0].rearrange("p n t -> p (n t)").bitcast(I32))
         obs_sb = keep.tile([P, PACK, V], F32, name="obs_sb")
@@ -107,28 +108,30 @@ def tile_picked_yenkf_half_po_kernel(tc, x_words, x_scales, w1, obs, w2, ens, of
             y_bank.append(bank)
 
         groups = BLOCK // D
-        sums = [keep.tile([P, groups, PACK], F32, name=f"sums{b}") for b in range(4)]
-        om = [keep.tile([P, groups, PACK], F32, name=f"om{b}") for b in range(4)]
+        sums = [keep.tile([P, 2 * groups, PACK], F32, name=f"sums{h}") for h in range(2)]
+        om = [keep.tile([P, 2 * groups, PACK], F32, name=f"om{h}") for h in range(2)]
         rr_bf = [keep.tile([P, HALF * PACK], BF16, name="rr_bf0", align_bytes=64)]
         rr_codes = [keep.tile([P, HALF], U32, name=f"rr_codes{h}", align_bytes=64) for h in range(2)]
         rr_scale = [keep.tile([P, HALF], U8, name=f"rr_scale{h}", align_bytes=64) for h in range(2)]
         update = [keep.tile([P, 2, S], F32, name=f"update{u}") for u in range(2)]
         result = [keep.tile([P, 2, S], F32, name=f"result{u}") for u in range(2)]
 
+        z_bank = [psum.tile([P, S], F32, name=f"z_bank{t}") for t in range(PACK)]
+
         def member_sums(b):
             nc.vector.tensor_reduce(
-                out=sums[b][:],
+                out=sums[b // 2][:, (b % 2) * groups : (b % 2 + 1) * groups, :],
                 in_=y_bank[b][:].rearrange("p t (v d) -> p v t d", d=D),
                 axis=mybir.AxisListType.X,
                 op=ALU.add,
             )
 
-        def innovation(b):
+        def innovation(h):
             nc.vector.scalar_tensor_tensor(
-                out=om[b][:],
-                in0=sums[b][:],
+                out=om[h][:],
+                in0=sums[h][:],
                 scalar=-1.0 / D,
-                in1=obs_sb[:, :, b * groups : (b + 1) * groups].rearrange("p t v -> p v t"),
+                in1=obs_sb[:, :, 2 * h * groups : 2 * (h + 1) * groups].rearrange("p t v -> p v t"),
                 op0=ALU.mult,
                 op1=ALU.add,
             )
@@ -137,40 +140,36 @@ def tile_picked_yenkf_half_po_kernel(tc, x_words, x_scales, w1, obs, w2, ens, of
             span = slice((b % 2) * BLOCK * PACK, (b % 2 + 1) * BLOCK * PACK)
             nc.vector.tensor_tensor(
                 out=rr_bf[b // 2][:, span].rearrange("p (v d t) -> p v d t", d=D, t=PACK),
-                in0=om[b][:].unsqueeze(2).broadcast_to([P, groups, D, PACK]),
+                in0=om[b // 2][:, (b % 2) * groups : (b % 2 + 1) * groups, :].unsqueeze(2).broadcast_to([P, groups, D, PACK]),
                 in1=y_bank[b][:].rearrange("p t (v d) -> p v d t", d=D),
                 op=ALU.subtract,
             )
 
         def second_product(h):
             nc.vector.quantize_mx(out=rr_codes[h][:].bitcast(FP8X4), scales=rr_scale[h][:], in_=rr_bf[h][:])
-            for u in range(2):
-                bank = psum.tile([P, 2, HALF], F32, name=f"z_bank{h}{u}")
-                for e in range(2):
-                    t = 2 * u + e
-                    nc.tensor.matmul_mx(
-                        out=bank[:, e, :],
-                        lhsT=w2_codes[:, t * P : (t + 1) * P].bitcast(FP8X4),
-                        lhsT_scale=w2_scale[:, t * P : (t + 1) * P],
-                        rhs=rr_codes[h][:].bitcast(FP8X4),
-                        rhs_scale=rr_scale[h][:],
-                        start=True,
-                        stop=True,
-                    )
-                nc.scalar.copy(out=update[u][:, :, h * HALF : (h + 1) * HALF], in_=bank[:])
+            cols = slice(h * HALF, (h + 1) * HALF)
+            for t in range(PACK):
+                nc.tensor.matmul_mx(
+                    out=z_bank[t][:, cols],
+                    lhsT=w2_codes[:, t * P : (t + 1) * P].bitcast(FP8X4),
+                    lhsT_scale=w2_scale[:, t * P : (t + 1) * P],
+                    rhs=rr_codes[h][:].bitcast(FP8X4),
+                    rhs_scale=rr_scale[h][:],
+                    start=True,
+                    stop=True,
+                )
+                nc.scalar.copy(out=update[t // 2][:, t % 2, cols], in_=z_bank[t][:, cols])
 
         member_sums(0)
         member_sums(1)
-        innovation(0)
         member_sums(2)
-        innovation(1)
-        residual(0)
+        innovation(0)
         member_sums(3)
+        residual(0)
+        innovation(1)
         residual(1)
-        innovation(2)
         nc.vector.quantize_mx(out=w2_codes[:].bitcast(FP8X4), scales=w2_scale[:], in_=w2_bf[:])
         rr_bf.append(keep.tile([P, HALF * PACK], BF16, name="rr_bf1", tag="bf_stage", align_bytes=64))
-        innovation(3)
         second_product(0)
         residual(2)
         residual(3)

@@ -25,23 +25,23 @@ def tile_picked_yenkf_half_po_kernel(tc, x_words, x_scales, w1, obs, w2, ens, of
     nc = tc.nc
     with ExitStack() as ctx:
         keep = ctx.enter_context(tc.tile_pool(name="keep", bufs=1))
+        shared = ctx.enter_context(tc.tile_pool(name="shared", bufs=1))
         psum = ctx.enter_context(tc.psum_pool(name="psum", bufs=1))
 
         offsets = keep.tile([P, S // LANES], U16, name="offsets")
-        nc.sync.dma_start(offsets[:], offs)
-
         x_scale_table = keep.tile([P, T], U8, name="x_scale_table", align_bytes=64)
         nc.vector.memset(x_scale_table[:, : T // 2].bitcast(I32), 0)
         nc.gpsimd.memset(x_scale_table[:, T // 2 :].bitcast(I32), 0)
+        w1_rows = w1.rearrange("(p j) c -> p j c", j=PACK)
+        w1_raw = [keep.tile([P, 2, H], F32, name=f"w1_raw{u}") for u in range(2)]
+        nc.sync.dma_start(out=w1_raw[0][:], in_=w1_rows[:, 0:2, :])
+        nc.sync.dma_start(offsets[:], offs)
         for q in range(4):
             nc.sync.dma_start(
                 out=x_scale_table[32 * q : 32 * q + 4, :].bitcast(I32),
                 in_=x_scales[0, 4 * q : 4 * q + 4, :].bitcast(I32),
             )
-        w1_rows = w1.rearrange("(p j) c -> p j c", j=PACK)
-        w1_raw = [keep.tile([P, 2, H], F32, name=f"w1_raw{u}") for u in range(2)]
-        for u in range(2):
-            nc.sync.dma_start(out=w1_raw[u][:], in_=w1_rows[:, 2 * u : 2 * u + 2, :])
+        nc.sync.dma_start(out=w1_raw[1][:], in_=w1_rows[:, 2:4, :])
         x_word_table = keep.tile([P, T], I32, name="x_word_table", align_bytes=64)
         nc.sync.dma_start(out=x_word_table[:], in_=x_words[0].rearrange("p n t -> p (n t)").bitcast(I32))
         obs_sb = keep.tile([P, PACK, V], F32, name="obs_sb")
@@ -60,24 +60,27 @@ def tile_picked_yenkf_half_po_kernel(tc, x_words, x_scales, w1, obs, w2, ens, of
 
         w1_bf = keep.tile([P, H * PACK], BF16, name="w1_bf", align_bytes=64)
 
-        def round_w1(u):
-            nc.vector.tensor_scalar(
-                out=w1_bf[:].rearrange("p (t m j) -> p m j t", t=PACK, j=PACK)[:, :, 2 * u : 2 * u + 2, :],
-                in0=w1_raw[u][:].rearrange("p j (m t) -> p m j t", t=PACK),
-                scalar1=0.5,
-                scalar2=None,
-                op0=ALU.mult,
-            )
-
-        round_w1(0)
+        w1_dealt = w1_bf[:].rearrange("p (t m j) -> p m j t", t=PACK, j=PACK)
+        nc.scalar.activation(
+            out=w1_dealt[:, :, 0:2, :],
+            in_=w1_raw[0][:].rearrange("p j (m t) -> p m j t", t=PACK),
+            func=mybir.ActivationFunctionType.Copy,
+            scale=0.5,
+        )
         x_scale = keep.tile([P, S], U8, name="x_scale", align_bytes=64)
         nc.vector.tensor_copy(x_scale[:], x_scale_table[:].indirect(offsets[:]))
-        round_w1(1)
+        nc.vector.tensor_scalar(
+            out=w1_dealt[:, :, 2:4, :],
+            in0=w1_raw[1][:].rearrange("p j (m t) -> p m j t", t=PACK),
+            scalar1=0.5,
+            scalar2=None,
+            op0=ALU.mult,
+        )
         w1_codes = keep.tile([P, H], U32, name="w1_codes", align_bytes=64)
         w1_scale = keep.tile([P, H], U8, name="w1_scale", align_bytes=64)
         nc.vector.quantize_mx(out=w1_codes[:].bitcast(FP8X4), scales=w1_scale[:], in_=w1_bf[:])
 
-        w2_bf = keep.tile([P, N * PACK], BF16, name="w2_bf", tag="bf_stage", align_bytes=64)
+        w2_bf = shared.tile([P, N * PACK], BF16, name="w2_bf", align_bytes=64, offset=0)
         nc.scalar.copy(
             out=w2_bf[:].rearrange("p (t m j) -> p m j t", t=PACK, j=PACK),
             in_=w2_raw[:].rearrange("p j (m t) -> p m j t", t=PACK),
@@ -110,11 +113,20 @@ def tile_picked_yenkf_half_po_kernel(tc, x_words, x_scales, w1, obs, w2, ens, of
         groups = BLOCK // D
         sums = [keep.tile([P, 2 * groups, PACK], F32, name=f"sums{h}") for h in range(2)]
         om = [keep.tile([P, 2 * groups, PACK], F32, name=f"om{h}") for h in range(2)]
-        rr_bf = [keep.tile([P, HALF * PACK], BF16, name="rr_bf0", align_bytes=64)]
-        rr_codes = [keep.tile([P, HALF], U32, name=f"rr_codes{h}", align_bytes=64) for h in range(2)]
+        rr_bf = [
+            keep.tile([P, HALF * PACK], BF16, name="rr_bf0", align_bytes=64),
+            shared.tile([P, HALF * PACK], BF16, name="rr_bf1", align_bytes=64, offset=0),
+        ]
+        rr_codes = [
+            shared.tile([P, HALF], U32, name="rr_codes0", align_bytes=64, offset=2048),
+            keep.tile([P, HALF], U32, name="rr_codes1", align_bytes=64),
+        ]
         rr_scale = [keep.tile([P, HALF], U8, name=f"rr_scale{h}", align_bytes=64) for h in range(2)]
         update = [keep.tile([P, 2, S], F32, name=f"update{u}") for u in range(2)]
-        result = [keep.tile([P, 2, S], F32, name=f"result{u}") for u in range(2)]
+        result = [
+            shared.tile([P, 2, S], F32, name="result0", align_bytes=64, offset=0),
+            keep.tile([P, 2, S], F32, name="result1"),
+        ]
 
         z_bank = [psum.tile([P, S], F32, name=f"z_bank{t}") for t in range(PACK)]
 
@@ -145,8 +157,14 @@ def tile_picked_yenkf_half_po_kernel(tc, x_words, x_scales, w1, obs, w2, ens, of
                 op=ALU.subtract,
             )
 
+        def quantise_residual(h, first, count):
+            nc.vector.quantize_mx(
+                out=rr_codes[h][:, first : first + count].bitcast(FP8X4),
+                scales=rr_scale[h][:, first : first + count],
+                in_=rr_bf[h][:, first * PACK : (first + count) * PACK],
+            )
+
         def second_product(h):
-            nc.vector.quantize_mx(out=rr_codes[h][:].bitcast(FP8X4), scales=rr_scale[h][:], in_=rr_bf[h][:])
             cols = slice(h * HALF, (h + 1) * HALF)
             for t in range(PACK):
                 nc.tensor.matmul_mx(
@@ -169,10 +187,12 @@ def tile_picked_yenkf_half_po_kernel(tc, x_words, x_scales, w1, obs, w2, ens, of
         innovation(1)
         residual(1)
         nc.vector.quantize_mx(out=w2_codes[:].bitcast(FP8X4), scales=w2_scale[:], in_=w2_bf[:])
-        rr_bf.append(keep.tile([P, HALF * PACK], BF16, name="rr_bf1", tag="bf_stage", align_bytes=64))
+        quantise_residual(0, 0, HALF)
         second_product(0)
         residual(2)
         residual(3)
+        quantise_residual(1, 0, BLOCK)
+        quantise_residual(1, BLOCK, BLOCK)
         second_product(1)
 
         out_rows = out_0.rearrange("(p t) c -> p t c", t=PACK)

@@ -60,18 +60,18 @@ def tile_picked_yenkf_half_po_kernel(tc, x_words, x_scales, w1, obs, w2, ens, of
 
         w1_bf = keep.tile([P, H * PACK], BF16, name="w1_bf", align_bytes=64)
 
-        w1_dealt = w1_bf[:].rearrange("p (t m j) -> p m j t", t=PACK, j=PACK)
+        w1_dealt = w1_bf[:].rearrange("p (t m j) -> p m t j", t=PACK, j=PACK)
         nc.scalar.activation(
-            out=w1_dealt[:, :, 0:2, :],
-            in_=w1_raw[0][:].rearrange("p j (m t) -> p m j t", t=PACK),
+            out=w1_dealt[:, :, :, 0:2],
+            in_=w1_raw[0][:].rearrange("p j (m t) -> p m t j", t=PACK),
             func=mybir.ActivationFunctionType.Copy,
             scale=0.5,
         )
         x_scale = keep.tile([P, S], U8, name="x_scale", align_bytes=64)
         nc.vector.tensor_copy(x_scale[:], x_scale_table[:].indirect(offsets[:]))
         nc.vector.tensor_scalar(
-            out=w1_dealt[:, :, 2:4, :],
-            in0=w1_raw[1][:].rearrange("p j (m t) -> p m j t", t=PACK),
+            out=w1_dealt[:, :, :, 2:4],
+            in0=w1_raw[1][:].rearrange("p j (m t) -> p m t j", t=PACK),
             scalar1=0.5,
             scalar2=None,
             op0=ALU.mult,
@@ -82,8 +82,8 @@ def tile_picked_yenkf_half_po_kernel(tc, x_words, x_scales, w1, obs, w2, ens, of
 
         w2_bf = shared.tile([P, N * PACK], BF16, name="w2_bf", align_bytes=64, offset=0)
         nc.scalar.copy(
-            out=w2_bf[:].rearrange("p (t m j) -> p m j t", t=PACK, j=PACK),
-            in_=w2_raw[:].rearrange("p j (m t) -> p m j t", t=PACK),
+            out=w2_bf[:].rearrange("p (t m j) -> p m t j", t=PACK, j=PACK),
+            in_=w2_raw[:].rearrange("p j (m t) -> p m t j", t=PACK),
         )
         w2_codes = keep.tile([P, N], U32, name="w2_codes", align_bytes=64)
         w2_scale = keep.tile([P, N], U8, name="w2_scale", align_bytes=64)

@@ -196,47 +196,55 @@ def tile_picked_yenkf_half_po_kernel(tc, x_words, x_scales, w1, obs, w2, ens, of
         second_product(1)
 
         out_rows = out_0.rearrange("(p t) c -> p t c", t=PACK)
-        out_bf = [keep.tile([P, HALF, PACK], BF16, name=f"out_bf{h}", align_bytes=64) for h in range(2)]
+        out_bf = keep.tile([P, S, PACK], BF16, name="out_bf", align_bytes=64)
         out_codes = keep.tile([P, S], U32, name="out_codes", align_bytes=64)
         out_scale = keep.tile([P, S], U8, name="out_scale", align_bytes=64)
         out_words = out_1[0].rearrange("p n t -> p (n t)").bitcast(I32)
 
-        def add_states(t, h):
-            cols = slice(h * HALF, (h + 1) * HALF)
+        def add_states(t, first, count):
+            cols = slice(first, first + count)
             nc.vector.tensor_tensor(
                 result[t // 2][:, t % 2, cols],
-                ens_table[t][:].indirect(half_list(h)),
+                ens_table[t][:].indirect(offsets[:, first // LANES : (first + count) // LANES]),
                 update[t // 2][:, t % 2, cols],
                 ALU.add,
             )
 
-        def round_pair(copy, u, h):
-            cols = slice(h * HALF, (h + 1) * HALF)
-            copy(out=out_bf[h][:, :, 2 * u : 2 * u + 2], in_=result[u][:, :, cols].rearrange("p e c -> p c e"))
+        def round_pair(copy, u, first, count):
+            cols = slice(first, first + count)
+            copy(out=out_bf[:, cols, 2 * u : 2 * u + 2], in_=result[u][:, :, cols].rearrange("p e c -> p c e"))
 
-        def quantise_result(h):
-            cols = slice(h * HALF, (h + 1) * HALF)
+        def quantise_result(first, count):
+            cols = slice(first, first + count)
             nc.vector.quantize_mx(
                 out=out_codes[:, cols].bitcast(FP8X4),
                 scales=out_scale[:, cols],
-                in_=out_bf[h][:].rearrange("p c t -> p (c t)"),
+                in_=out_bf[:, cols, :].rearrange("p c t -> p (c t)"),
             )
+
+        def store_words(first, count):
+            cols = slice(first, first + count)
             nc.sync.dma_start(out=out_words[:, cols], in_=out_codes[:, cols].bitcast(I32))
 
         for h in range(2):
-            add_states(0, h)
-            add_states(1, h)
-            round_pair(nc.scalar.copy, 0, h)
+            add_states(0, h * HALF, HALF)
+            add_states(1, h * HALF, HALF)
+            round_pair(nc.scalar.copy, 0, h * HALF, HALF)
         nc.sync.dma_start(out=out_rows[:, 0:2, :], in_=result[0][:])
-        nc.vector.tensor_tensor(result[1][:, 0, :], ens_table[2][:].indirect(offsets[:]), update[1][:, 0, :], ALU.add)
+        add_states(2, 0, S)
         nc.sync.dma_start(out=out_rows[:, 2, :], in_=result[1][:, 0, :])
-        add_states(3, 0)
-        round_pair(nc.scalar.copy, 1, 0)
-        add_states(3, 1)
-        nc.sync.dma_start(out=out_rows[:, 3, :], in_=result[1][:, 1, :])
-        round_pair(nc.vector.tensor_copy, 1, 1)
-        quantise_result(0)
-        quantise_result(1)
+        blocks = S // BLOCK
+        for b in range(blocks):
+            add_states(3, b * BLOCK, BLOCK)
+            if b < blocks - 1:
+                round_pair(nc.scalar.copy, 1, b * BLOCK, BLOCK)
+            if b % 2 == 1:
+                cols = slice((b - 1) * BLOCK, (b + 1) * BLOCK)
+                nc.sync.dma_start(out=out_rows[:, 3, cols], in_=result[1][:, 1, cols])
+        round_pair(nc.vector.tensor_copy, 1, S - BLOCK, BLOCK)
+        for h in range(2):
+            quantise_result(h * HALF, HALF)
+            store_words(h * HALF, HALF)
         for q in range(4):
             queue = nc.scalar if q % 2 == 0 else nc.sync
             queue.dma_start(

@@ -51,7 +51,10 @@ def tile_picked_yenkf_half_po_kernel(tc, x_words, x_scales, w1, obs, w2, ens, of
         ens_rows = ens.rearrange("(p t) c -> p t c", t=PACK)
         ens_table = []
         for t in range(PACK):
-            table = keep.tile([P, T], F32, name=f"ens_table{t}")
+            if t in (1, 2):
+                table = shared.tile([P, T], F32, name=f"ens_table{t}", align_bytes=64, offset=4096 + (t - 1) * 4 * T)
+            else:
+                table = keep.tile([P, T], F32, name=f"ens_table{t}")
             nc.sync.dma_start(out=table[:], in_=ens_rows[:, t, :])
             ens_table.append(table)
 
@@ -69,12 +72,19 @@ def tile_picked_yenkf_half_po_kernel(tc, x_words, x_scales, w1, obs, w2, ens, of
         )
         x_scale = keep.tile([P, S], U8, name="x_scale", align_bytes=64)
         nc.vector.tensor_copy(x_scale[:], x_scale_table[:].indirect(offsets[:]))
+        w1_late = w1_raw[1][:].rearrange("p j (m t) -> p m t j", t=PACK)
         nc.vector.tensor_scalar(
-            out=w1_dealt[:, :, :, 2:4],
-            in0=w1_raw[1][:].rearrange("p j (m t) -> p m t j", t=PACK),
+            out=w1_dealt[:, : P // 2, :, 2:4],
+            in0=w1_late[:, : P // 2],
             scalar1=0.5,
             scalar2=None,
             op0=ALU.mult,
+        )
+        nc.scalar.activation(
+            out=w1_dealt[:, P // 2 :, :, 2:4],
+            in_=w1_late[:, P // 2 :],
+            func=mybir.ActivationFunctionType.Copy,
+            scale=0.5,
         )
         w1_codes = keep.tile([P, H], U32, name="w1_codes", align_bytes=64)
         w1_scale = keep.tile([P, H], U8, name="w1_scale", align_bytes=64)
@@ -122,13 +132,19 @@ def tile_picked_yenkf_half_po_kernel(tc, x_words, x_scales, w1, obs, w2, ens, of
             keep.tile([P, HALF], U32, name="rr_codes1", align_bytes=64),
         ]
         rr_scale = [keep.tile([P, HALF], U8, name=f"rr_scale{h}", align_bytes=64) for h in range(2)]
-        update = [keep.tile([P, 2, S], F32, name=f"update{u}") for u in range(2)]
+        picked = keep.tile([P, PACK - 1, S], F32, name="picked")
+        for t in range(PACK - 1):
+            nc.scalar.activation(
+                out=picked[:, t, :],
+                in_=ens_table[t][:].indirect(offsets[:]),
+                func=mybir.ActivationFunctionType.Copy,
+            )
         result = [
             shared.tile([P, 2, S], F32, name="result0", align_bytes=64, offset=0),
             keep.tile([P, 2, S], F32, name="result1"),
         ]
 
-        z_bank = [psum.tile([P, S], F32, name=f"z_bank{t}") for t in range(PACK)]
+        z_bank = [[psum.tile([P, 2, HALF], F32, name=f"z_bank{h}{u}") for u in range(2)] for h in range(2)]
 
         def member_sums(b):
             nc.vector.tensor_reduce(
@@ -165,10 +181,9 @@ def tile_picked_yenkf_half_po_kernel(tc, x_words, x_scales, w1, obs, w2, ens, of
             )
 
         def second_product(h):
-            cols = slice(h * HALF, (h + 1) * HALF)
             for t in range(PACK):
                 nc.tensor.matmul_mx(
-                    out=z_bank[t][:, cols],
+                    out=z_bank[h][t // 2][:, t % 2, :],
                     lhsT=w2_codes[:, t * P : (t + 1) * P].bitcast(FP8X4),
                     lhsT_scale=w2_scale[:, t * P : (t + 1) * P],
                     rhs=rr_codes[h][:].bitcast(FP8X4),
@@ -176,7 +191,6 @@ def tile_picked_yenkf_half_po_kernel(tc, x_words, x_scales, w1, obs, w2, ens, of
                     start=True,
                     stop=True,
                 )
-                nc.scalar.copy(out=update[t // 2][:, t % 2, cols], in_=z_bank[t][:, cols])
 
         member_sums(0)
         member_sums(1)
@@ -196,46 +210,47 @@ def tile_picked_yenkf_half_po_kernel(tc, x_words, x_scales, w1, obs, w2, ens, of
         second_product(1)
 
         out_rows = out_0.rearrange("(p t) c -> p t c", t=PACK)
-        out_bf = keep.tile([P, S, PACK], BF16, name="out_bf", align_bytes=64)
+        update = [
+            shared.tile([P, HALF], F32, name=f"update{h}", align_bytes=64, offset=4096 + h * 4 * T) for h in range(2)
+        ]
+        out_bf = [
+            keep.tile([P, HALF, PACK], BF16, name="out_bf0", align_bytes=64),
+            shared.tile([P, HALF, PACK], BF16, name="out_bf1", align_bytes=64, offset=4096 + 4 * T + 4 * HALF),
+        ]
         out_codes = keep.tile([P, S], U32, name="out_codes", align_bytes=64)
         out_scale = keep.tile([P, S], U8, name="out_scale", align_bytes=64)
         out_words = out_1[0].rearrange("p n t -> p (n t)").bitcast(I32)
 
-        def add_states(t, first, count):
-            cols = slice(first, first + count)
+        def add_last_states(first, count):
+            place = first % HALF
             nc.vector.tensor_tensor(
-                result[t // 2][:, t % 2, cols],
-                ens_table[t][:].indirect(offsets[:, first // LANES : (first + count) // LANES]),
-                update[t // 2][:, t % 2, cols],
+                result[1][:, 1, first : first + count],
+                ens_table[3][:].indirect(offsets[:, first // LANES : (first + count) // LANES]),
+                update[first // HALF][:, place : place + count],
                 ALU.add,
             )
 
         def round_pair(copy, u, first, count):
-            cols = slice(first, first + count)
-            copy(out=out_bf[:, cols, 2 * u : 2 * u + 2], in_=result[u][:, :, cols].rearrange("p e c -> p c e"))
-
-        def quantise_result(first, count):
-            cols = slice(first, first + count)
-            nc.vector.quantize_mx(
-                out=out_codes[:, cols].bitcast(FP8X4),
-                scales=out_scale[:, cols],
-                in_=out_bf[:, cols, :].rearrange("p c t -> p (c t)"),
+            place = first % HALF
+            copy(
+                out=out_bf[first // HALF][:, place : place + count, 2 * u : 2 * u + 2],
+                in_=result[u][:, :, first : first + count].rearrange("p e c -> p c e"),
             )
 
-        def store_words(first, count):
-            cols = slice(first, first + count)
-            nc.sync.dma_start(out=out_words[:, cols], in_=out_codes[:, cols].bitcast(I32))
-
         for h in range(2):
-            add_states(0, h * HALF, HALF)
-            add_states(1, h * HALF, HALF)
-            round_pair(nc.scalar.copy, 0, h * HALF, HALF)
+            cols = slice(h * HALF, (h + 1) * HALF)
+            nc.scalar.copy(out=update[h][:], in_=z_bank[h][1][:, 1, :])
+            nc.vector.tensor_tensor(result[0][:, :, cols], picked[:, 0:2, cols], z_bank[h][0][:], ALU.add)
         nc.sync.dma_start(out=out_rows[:, 0:2, :], in_=result[0][:])
-        add_states(2, 0, S)
+        round_pair(nc.vector.tensor_copy, 0, 0, HALF)
+        round_pair(nc.scalar.copy, 0, HALF, HALF)
+        for h in range(2):
+            cols = slice(h * HALF, (h + 1) * HALF)
+            nc.vector.tensor_tensor(result[1][:, 0, cols], picked[:, 2, cols], z_bank[h][1][:, 0, :], ALU.add)
         nc.sync.dma_start(out=out_rows[:, 2, :], in_=result[1][:, 0, :])
         blocks = S // BLOCK
         for b in range(blocks):
-            add_states(3, b * BLOCK, BLOCK)
+            add_last_states(b * BLOCK, BLOCK)
             if b < blocks - 1:
                 round_pair(nc.scalar.copy, 1, b * BLOCK, BLOCK)
             if b % 2 == 1:
@@ -243,8 +258,13 @@ def tile_picked_yenkf_half_po_kernel(tc, x_words, x_scales, w1, obs, w2, ens, of
                 nc.sync.dma_start(out=out_rows[:, 3, cols], in_=result[1][:, 1, cols])
         round_pair(nc.vector.tensor_copy, 1, S - BLOCK, BLOCK)
         for h in range(2):
-            quantise_result(h * HALF, HALF)
-            store_words(h * HALF, HALF)
+            cols = slice(h * HALF, (h + 1) * HALF)
+            nc.vector.quantize_mx(
+                out=out_codes[:, cols].bitcast(FP8X4),
+                scales=out_scale[:, cols],
+                in_=out_bf[h][:].rearrange("p c t -> p (c t)"),
+            )
+            nc.sync.dma_start(out=out_words[:, cols], in_=out_codes[:, cols].bitcast(I32))
         for q in range(4):
             queue = nc.scalar if q % 2 == 0 else nc.sync
             queue.dma_start(

@@ -210,61 +210,62 @@ def tile_picked_yenkf_half_po_kernel(tc, x_words, x_scales, w1, obs, w2, ens, of
         second_product(1)
 
         out_rows = out_0.rearrange("(p t) c -> p t c", t=PACK)
-        update = [
-            shared.tile([P, HALF], F32, name=f"update{h}", align_bytes=64, offset=4096 + h * 4 * T) for h in range(2)
-        ]
-        out_bf = [
-            keep.tile([P, HALF, PACK], BF16, name="out_bf0", align_bytes=64),
-            shared.tile([P, HALF, PACK], BF16, name="out_bf1", align_bytes=64, offset=4096 + 4 * T + 4 * HALF),
-        ]
+        update = shared.tile([P, HALF], F32, name="update", align_bytes=64, offset=4096)
+        picked_last = keep.tile([P, HALF], F32, name="picked_last")
+        out_bf = keep.tile([P, S, PACK], BF16, name="out_bf", align_bytes=64)
         out_codes = keep.tile([P, S], U32, name="out_codes", align_bytes=64)
         out_scale = keep.tile([P, S], U8, name="out_scale", align_bytes=64)
         out_words = out_1[0].rearrange("p n t -> p (n t)").bitcast(I32)
 
-        def add_last_states(first, count):
-            place = first % HALF
-            nc.vector.tensor_tensor(
-                result[1][:, 1, first : first + count],
-                ens_table[3][:].indirect(offsets[:, first // LANES : (first + count) // LANES]),
-                update[first // HALF][:, place : place + count],
-                ALU.add,
-            )
+        def block(b):
+            return slice(b * BLOCK, (b + 1) * BLOCK)
 
-        def round_pair(copy, u, first, count):
-            place = first % HALF
-            copy(
-                out=out_bf[first // HALF][:, place : place + count, 2 * u : 2 * u + 2],
-                in_=result[u][:, :, first : first + count].rearrange("p e c -> p c e"),
-            )
+        def block_list(b):
+            return offsets[:, b * (BLOCK // LANES) : (b + 1) * (BLOCK // LANES)]
 
-        for h in range(2):
-            cols = slice(h * HALF, (h + 1) * HALF)
-            nc.scalar.copy(out=update[h][:], in_=z_bank[h][1][:, 1, :])
-            nc.vector.tensor_tensor(result[0][:, :, cols], picked[:, 0:2, cols], z_bank[h][0][:], ALU.add)
-        nc.sync.dma_start(out=out_rows[:, 0:2, :], in_=result[0][:])
-        round_pair(nc.vector.tensor_copy, 0, 0, HALF)
-        round_pair(nc.scalar.copy, 0, HALF, HALF)
-        for h in range(2):
-            cols = slice(h * HALF, (h + 1) * HALF)
-            nc.vector.tensor_tensor(result[1][:, 0, cols], picked[:, 2, cols], z_bank[h][1][:, 0, :], ALU.add)
-        nc.sync.dma_start(out=out_rows[:, 2, :], in_=result[1][:, 0, :])
-        blocks = S // BLOCK
-        for b in range(blocks):
-            add_last_states(b * BLOCK, BLOCK)
-            if b < blocks - 1:
-                round_pair(nc.scalar.copy, 1, b * BLOCK, BLOCK)
-            if b % 2 == 1:
-                cols = slice((b - 1) * BLOCK, (b + 1) * BLOCK)
-                nc.sync.dma_start(out=out_rows[:, 3, cols], in_=result[1][:, 1, cols])
-        round_pair(nc.vector.tensor_copy, 1, S - BLOCK, BLOCK)
-        for h in range(2):
-            cols = slice(h * HALF, (h + 1) * HALF)
+        def round_pair(copy, u, cols):
+            copy(out=out_bf[:, cols, 2 * u : 2 * u + 2], in_=result[u][:, :, cols].rearrange("p e c -> p c e"))
+
+        def quantise_result(cols):
             nc.vector.quantize_mx(
                 out=out_codes[:, cols].bitcast(FP8X4),
                 scales=out_scale[:, cols],
-                in_=out_bf[h][:].rearrange("p c t -> p (c t)"),
+                in_=out_bf[:, cols, :].rearrange("p c t -> p (c t)"),
             )
-            nc.sync.dma_start(out=out_words[:, cols], in_=out_codes[:, cols].bitcast(I32))
+
+        halves = [slice(h * HALF, (h + 1) * HALF) for h in range(2)]
+        nc.scalar.copy(out=update[:], in_=z_bank[0][1][:, 1, :])
+        for h, cols in enumerate(halves):
+            nc.vector.tensor_tensor(result[0][:, :, cols], picked[:, 0:2, cols], z_bank[h][0][:], ALU.add)
+        nc.sync.dma_start(out=out_rows[:, 0:2, :], in_=result[0][:])
+        for cols in halves:
+            round_pair(nc.vector.tensor_copy, 0, cols)
+        for h, cols in enumerate(halves):
+            nc.vector.tensor_tensor(result[1][:, 0, cols], picked[:, 2, cols], z_bank[h][1][:, 0, :], ALU.add)
+        nc.sync.dma_start(out=out_rows[:, 2, :], in_=result[1][:, 0, :])
+        for b in (2, 3):
+            nc.scalar.activation(
+                out=picked_last[:, block(b - 2)],
+                in_=ens_table[3][:].indirect(block_list(b)),
+                func=mybir.ActivationFunctionType.Copy,
+            )
+        for b in (0, 1):
+            nc.vector.tensor_tensor(
+                result[1][:, 1, block(b)], ens_table[3][:].indirect(block_list(b)), update[:, block(b)], ALU.add
+            )
+            round_pair(nc.scalar.copy, 1, block(b))
+        nc.sync.dma_start(out=out_rows[:, 3, halves[0]], in_=result[1][:, 1, halves[0]])
+        for b in (2, 3):
+            nc.vector.tensor_tensor(
+                result[1][:, 1, block(b)], picked_last[:, block(b - 2)], z_bank[1][1][:, 1, block(b - 2)], ALU.add
+            )
+        nc.sync.dma_start(out=out_rows[:, 3, halves[1]], in_=result[1][:, 1, halves[1]])
+        for b in (2, 3):
+            round_pair(nc.vector.tensor_copy, 1, block(b))
+        for b in (0, 2, 1, 3):
+            quantise_result(block(b))
+            if b % 2 == 1:
+                nc.sync.dma_start(out=out_words[:, halves[b // 2]], in_=out_codes[:, halves[b // 2]].bitcast(I32))
         for q in range(4):
             queue = nc.scalar if q % 2 == 0 else nc.sync
             queue.dma_start(

@@ -19,6 +19,7 @@ PACK = 4
 LANES = 16
 BLOCK = 128
 HALF = 256
+BANK = 2048
 
 
 def tile_picked_yenkf_half_po_kernel(tc, x_words, x_scales, w1, obs, w2, ens, offs, out_0, out_1, out_2):
@@ -72,6 +73,11 @@ def tile_picked_yenkf_half_po_kernel(tc, x_words, x_scales, w1, obs, w2, ens, of
         )
         x_scale = keep.tile([P, S], U8, name="x_scale", align_bytes=64)
         nc.vector.tensor_copy(x_scale[:], x_scale_table[:].indirect(offsets[:]))
+        x_scale_dealt = keep.tile([P, HALF], U8, name="x_scale_dealt", align_bytes=64)
+        nc.vector.tensor_copy(
+            x_scale_dealt[:].bitcast(I32).rearrange("p (e v) -> p e v", e=2),
+            x_scale[:, HALF:].bitcast(I32).rearrange("p (v e) -> p e v", e=2),
+        )
         w1_late = w1_raw[1][:].rearrange("p j (m t) -> p m t j", t=PACK)
         nc.vector.tensor_scalar(
             out=w1_dealt[:, : P // 2, :, 2:4],
@@ -98,27 +104,37 @@ def tile_picked_yenkf_half_po_kernel(tc, x_words, x_scales, w1, obs, w2, ens, of
         w2_codes = keep.tile([P, N], U32, name="w2_codes", align_bytes=64)
         w2_scale = keep.tile([P, N], U8, name="w2_scale", align_bytes=64)
 
-        x_codes = []
-        for h in range(2):
-            picked = keep.tile([P, HALF], U32, name=f"x_codes{h}", align_bytes=64)
-            nc.vector.tensor_copy(picked[:], x_word_table[:].bitcast(U32).indirect(half_list(h)))
-            x_codes.append(picked)
+        x_codes = [keep.tile([P, HALF], U32, name=f"x_codes{h}", align_bytes=64) for h in range(2)]
+        nc.vector.tensor_copy(x_codes[0][:], x_word_table[:].bitcast(U32).indirect(half_list(0)))
+        nc.vector.tensor_copy(
+            x_codes[1][:].rearrange("p (e v d) -> p v e d", e=2, d=D // 2),
+            x_word_table[:].bitcast(U32).indirect(half_list(1)),
+        )
+        x_scales_of = [x_scale, x_scale_dealt]
 
-        y_bank = []
-        for b in range(S // BLOCK):
-            bank = psum.tile([P, PACK, BLOCK], F32, name=f"y_bank{b}")
+        def first_product(out, t, b, start, stop):
             cols = slice((b % 2) * BLOCK, (b % 2 + 1) * BLOCK)
+            nc.tensor.matmul_mx(
+                out=out[:, t, :],
+                lhsT=w1_codes[:, t * P : (t + 1) * P].bitcast(FP8X4),
+                lhsT_scale=w1_scale[:, t * P : (t + 1) * P],
+                rhs=x_codes[b // 2][:, cols].bitcast(FP8X4),
+                rhs_scale=x_scales_of[b // 2][:, cols],
+                start=start,
+                stop=stop,
+            )
+
+        y_bank = [psum.tile([P, PACK, BLOCK], F32, name=f"y_bank{b}", offset=b * BANK) for b in range(S // BLOCK)]
+        pair_bank = psum.tile([P, PACK, BLOCK], F32, name="pair_bank", offset=4 * BANK)
+        for b in (0, 1):
             for t in range(PACK):
-                nc.tensor.matmul_mx(
-                    out=bank[:, t, :],
-                    lhsT=w1_codes[:, t * P : (t + 1) * P].bitcast(FP8X4),
-                    lhsT_scale=w1_scale[:, t * P : (t + 1) * P],
-                    rhs=x_codes[b // 2][:, cols].bitcast(FP8X4),
-                    rhs_scale=x_scale[:, b * BLOCK : (b + 1) * BLOCK],
-                    start=True,
-                    stop=True,
-                )
-            y_bank.append(bank)
+                first_product(y_bank[b], t, b, True, True)
+        for t in range(PACK):
+            first_product(pair_bank, t, 2, True, False)
+            first_product(pair_bank, t, 3, False, True)
+        for b in (2, 3):
+            for t in range(PACK):
+                first_product(y_bank[b], t, b, True, True)
 
         groups = BLOCK // D
         sums = [keep.tile([P, 2 * groups, PACK], F32, name=f"sums{h}") for h in range(2)]
@@ -144,7 +160,10 @@ def tile_picked_yenkf_half_po_kernel(tc, x_words, x_scales, w1, obs, w2, ens, of
             keep.tile([P, 2, S], F32, name="result1"),
         ]
 
-        z_bank = [[psum.tile([P, 2, HALF], F32, name=f"z_bank{h}{u}") for u in range(2)] for h in range(2)]
+        z_bank = [
+            [psum.tile([P, 2, HALF], F32, name=f"z_bank{h}{u}", offset=((2 * h + u + 4) * BANK if h + u else 0)) for u in range(2)]
+            for h in range(2)
+        ]
 
         def member_sums(b):
             nc.vector.tensor_reduce(
@@ -154,12 +173,29 @@ def tile_picked_yenkf_half_po_kernel(tc, x_words, x_scales, w1, obs, w2, ens, of
                 op=ALU.add,
             )
 
-        def innovation(h):
+        def member_sums_of_pairs():
+            nc.vector.tensor_reduce(
+                out=sums[1][:],
+                in_=pair_bank[:].rearrange("p t (v d) -> p v t d", d=D // 2),
+                axis=mybir.AxisListType.X,
+                op=ALU.add,
+            )
+
+        def residual_dealt(b, e):
+            span = slice(b * groups, (b + 1) * groups)
+            nc.vector.tensor_tensor(
+                out=rr_bf[1][:].rearrange("p (v e d t) -> p v e d t", e=2, d=D // 2, t=PACK)[:, span, e],
+                in0=om[1][:, span, :].unsqueeze(2).broadcast_to([P, groups, D // 2, PACK]),
+                in1=y_bank[2 + e][:].rearrange("p t (v d) -> p v d t", d=D // 2)[:, span],
+                op=ALU.subtract,
+            )
+
+        def innovation(h, first, count):
             nc.vector.scalar_tensor_tensor(
-                out=om[h][:],
-                in0=sums[h][:],
+                out=om[h][:, first : first + count, :],
+                in0=sums[h][:, first : first + count, :],
                 scalar=-1.0 / D,
-                in1=obs_sb[:, :, 2 * h * groups : 2 * (h + 1) * groups].rearrange("p t v -> p v t"),
+                in1=obs_sb[:, :, 2 * h * groups + first : 2 * h * groups + first + count].rearrange("p t v -> p v t"),
                 op0=ALU.mult,
                 op1=ALU.add,
             )
@@ -194,17 +230,18 @@ def tile_picked_yenkf_half_po_kernel(tc, x_words, x_scales, w1, obs, w2, ens, of
 
         member_sums(0)
         member_sums(1)
-        member_sums(2)
-        innovation(0)
-        member_sums(3)
+        innovation(0, 0, groups)
+        innovation(0, groups, groups)
         residual(0)
-        innovation(1)
+        member_sums_of_pairs()
         residual(1)
+        innovation(1, 0, 2 * groups)
         nc.vector.quantize_mx(out=w2_codes[:].bitcast(FP8X4), scales=w2_scale[:], in_=w2_bf[:])
         quantise_residual(0, 0, HALF)
         second_product(0)
-        residual(2)
-        residual(3)
+        for b in range(2):
+            for e in range(2):
+                residual_dealt(b, e)
         quantise_residual(1, 0, BLOCK)
         quantise_residual(1, BLOCK, BLOCK)
         second_product(1)
@@ -212,7 +249,14 @@ def tile_picked_yenkf_half_po_kernel(tc, x_words, x_scales, w1, obs, w2, ens, of
         out_rows = out_0.rearrange("(p t) c -> p t c", t=PACK)
         update = shared.tile([P, HALF], F32, name="update", align_bytes=64, offset=4096)
         picked_last = keep.tile([P, HALF], F32, name="picked_last")
-        out_bf = keep.tile([P, S, PACK], BF16, name="out_bf", align_bytes=64)
+        out_bf_first = shared.tile([P, BLOCK, PACK], BF16, name="out_bf_first", align_bytes=64, offset=4096 + 4 * T)
+        out_bf_rest = keep.tile([P, S - BLOCK, PACK], BF16, name="out_bf_rest", align_bytes=64)
+
+        def staged(cols):
+            if cols.start < BLOCK:
+                return out_bf_first[:, cols, :]
+            return out_bf_rest[:, cols.start - BLOCK : cols.stop - BLOCK, :]
+
         out_codes = keep.tile([P, S], U32, name="out_codes", align_bytes=64)
         out_scale = keep.tile([P, S], U8, name="out_scale", align_bytes=64)
         out_words = out_1[0].rearrange("p n t -> p (n t)").bitcast(I32)
@@ -224,13 +268,13 @@ def tile_picked_yenkf_half_po_kernel(tc, x_words, x_scales, w1, obs, w2, ens, of
             return offsets[:, b * (BLOCK // LANES) : (b + 1) * (BLOCK // LANES)]
 
         def round_pair(copy, u, cols):
-            copy(out=out_bf[:, cols, 2 * u : 2 * u + 2], in_=result[u][:, :, cols].rearrange("p e c -> p c e"))
+            copy(out=staged(cols)[:, :, 2 * u : 2 * u + 2], in_=result[u][:, :, cols].rearrange("p e c -> p c e"))
 
         def quantise_result(cols):
             nc.vector.quantize_mx(
                 out=out_codes[:, cols].bitcast(FP8X4),
                 scales=out_scale[:, cols],
-                in_=out_bf[:, cols, :].rearrange("p c t -> p (c t)"),
+                in_=staged(cols).rearrange("p c t -> p (c t)"),
             )
 
         halves = [slice(h * HALF, (h + 1) * HALF) for h in range(2)]
@@ -238,8 +282,9 @@ def tile_picked_yenkf_half_po_kernel(tc, x_words, x_scales, w1, obs, w2, ens, of
         for h, cols in enumerate(halves):
             nc.vector.tensor_tensor(result[0][:, :, cols], picked[:, 0:2, cols], z_bank[h][0][:], ALU.add)
         nc.sync.dma_start(out=out_rows[:, 0:2, :], in_=result[0][:])
-        for cols in halves:
-            round_pair(nc.vector.tensor_copy, 0, cols)
+        round_pair(nc.scalar.copy, 0, block(0))
+        round_pair(nc.vector.tensor_copy, 0, block(1))
+        round_pair(nc.vector.tensor_copy, 0, halves[1])
         for h, cols in enumerate(halves):
             nc.vector.tensor_tensor(result[1][:, 0, cols], picked[:, 2, cols], z_bank[h][1][:, 0, :], ALU.add)
         nc.sync.dma_start(out=out_rows[:, 2, :], in_=result[1][:, 0, :])

@@ -124,17 +124,14 @@ def tile_picked_yenkf_half_po_kernel(tc, x_words, x_scales, w1, obs, w2, ens, of
                 stop=stop,
             )
 
-        y_bank = [psum.tile([P, PACK, BLOCK], F32, name=f"y_bank{b}", offset=b * BANK) for b in range(S // BLOCK)]
-        pair_bank = psum.tile([P, PACK, BLOCK], F32, name="pair_bank", offset=4 * BANK)
+        y_bank = [psum.tile([P, PACK, BLOCK], F32, name=f"y_bank{b}", offset=b * BANK) for b in range(2)]
+        pair_bank = psum.tile([P, PACK, BLOCK], F32, name="pair_bank", offset=2 * BANK)
         for b in (0, 1):
             for t in range(PACK):
                 first_product(y_bank[b], t, b, True, True)
         for t in range(PACK):
             first_product(pair_bank, t, 2, True, False)
             first_product(pair_bank, t, 3, False, True)
-        for b in (2, 3):
-            for t in range(PACK):
-                first_product(y_bank[b], t, b, True, True)
 
         groups = BLOCK // D
         sums = [keep.tile([P, 2 * groups, PACK], F32, name=f"sums{h}") for h in range(2)]
@@ -161,7 +158,7 @@ def tile_picked_yenkf_half_po_kernel(tc, x_words, x_scales, w1, obs, w2, ens, of
         ]
 
         z_bank = [
-            [psum.tile([P, 2, HALF], F32, name=f"z_bank{h}{u}", offset=((2 * h + u + 4) * BANK if h + u else 0)) for u in range(2)]
+            [psum.tile([P, 2, HALF], F32, name=f"z_bank{h}{u}", offset=(2 * h + u + 3) * BANK) for u in range(2)]
             for h in range(2)
         ]
 
@@ -236,6 +233,11 @@ def tile_picked_yenkf_half_po_kernel(tc, x_words, x_scales, w1, obs, w2, ens, of
         member_sums_of_pairs()
         residual(1)
         innovation(1, 0, 2 * groups)
+        for b in (3, 2):
+            bank = psum.tile([P, PACK, BLOCK], F32, name=f"y_bank{b}", offset=(b - 1) * BANK)
+            for t in range(PACK):
+                first_product(bank, t, b, True, True)
+            y_bank.insert(2, bank)
         nc.vector.quantize_mx(out=w2_codes[:].bitcast(FP8X4), scales=w2_scale[:], in_=w2_bf[:])
         quantise_residual(0, 0, HALF)
         second_product(0)
@@ -309,8 +311,11 @@ def tile_picked_yenkf_half_po_kernel(tc, x_words, x_scales, w1, obs, w2, ens, of
             round_pair(nc.vector.tensor_copy, 1, block(b))
         for b in (0, 2, 1, 3):
             quantise_result(block(b))
-            if b % 2 == 1:
-                nc.sync.dma_start(out=out_words[:, halves[b // 2]], in_=out_codes[:, halves[b // 2]].bitcast(I32))
+            if b >= 2:
+                nc.sync.dma_start(
+                    out=out_words.rearrange("p (h e c) -> p h e c", h=2, e=2)[:, :, b - 2, :],
+                    in_=out_codes[:].bitcast(I32).rearrange("p (h e c) -> p h e c", h=2, e=2)[:, :, b - 2, :],
+                )
         for q in range(4):
             queue = nc.scalar if q % 2 == 0 else nc.sync
             queue.dma_start(

@@ -153,7 +153,7 @@ def tile_picked_yenkf_half_po_kernel(tc, x_words, x_scales, w1, obs, w2, ens, of
                 func=mybir.ActivationFunctionType.Copy,
             )
         result = [
-            shared.tile([P, 2, S], F32, name="result0", align_bytes=64, offset=0),
+            keep.tile([P, 2, S], F32, name="result0"),
             keep.tile([P, 2, S], F32, name="result1"),
         ]
 
@@ -317,8 +317,7 @@ def tile_picked_yenkf_half_po_kernel(tc, x_words, x_scales, w1, obs, w2, ens, of
                     in_=out_codes[:].bitcast(I32).rearrange("p (h e c) -> p h e c", h=2, e=2)[:, :, b - 2, :],
                 )
         for q in range(4):
-            queue = nc.scalar if q % 2 == 0 else nc.sync
-            queue.dma_start(
+            nc.sync.dma_start(
                 out=out_2[0, 4 * q : 4 * q + 4, :].bitcast(I32),
                 in_=out_scale[32 * q : 32 * q + 4, :].bitcast(I32),
             )

@@ -250,7 +250,7 @@ def tile_picked_yenkf_half_po_kernel(tc, x_words, x_scales, w1, obs, w2, ens, of
 
         out_rows = out_0.rearrange("(p t) c -> p t c", t=PACK)
         update = shared.tile([P, HALF], F32, name="update", align_bytes=64, offset=4096)
-        picked_last = keep.tile([P, HALF], F32, name="picked_last")
+        picked_last = shared.tile([P, HALF], F32, name="picked_last", align_bytes=64, offset=4096 + 2 * 4 * T)
         out_bf_first = shared.tile([P, BLOCK, PACK], BF16, name="out_bf_first", align_bytes=64, offset=4096 + 4 * T)
         out_bf_rest = keep.tile([P, S - BLOCK, PACK], BF16, name="out_bf_rest", align_bytes=64)
 
@@ -259,7 +259,6 @@ def tile_picked_yenkf_half_po_kernel(tc, x_words, x_scales, w1, obs, w2, ens, of
                 return out_bf_first[:, cols, :]
             return out_bf_rest[:, cols.start - BLOCK : cols.stop - BLOCK, :]
 
-        out_codes = keep.tile([P, S], U32, name="out_codes", align_bytes=64)
         out_scale = keep.tile([P, S], U8, name="out_scale", align_bytes=64)
         out_words = out_1[0].rearrange("p n t -> p (n t)").bitcast(I32)
 
@@ -272,11 +271,11 @@ def tile_picked_yenkf_half_po_kernel(tc, x_words, x_scales, w1, obs, w2, ens, of
         def round_pair(copy, u, cols):
             copy(out=staged(cols)[:, :, 2 * u : 2 * u + 2], in_=result[u][:, :, cols].rearrange("p e c -> p c e"))
 
-        def quantise_result(cols):
+        def quantise_result(b):
             nc.vector.quantize_mx(
-                out=out_codes[:, cols].bitcast(FP8X4),
-                scales=out_scale[:, cols],
-                in_=staged(cols).rearrange("p c t -> p (c t)"),
+                out=out_codes[b % 2][:, b // 2, :].bitcast(FP8X4),
+                scales=out_scale[:, block(b)],
+                in_=staged(block(b)).rearrange("p c t -> p (c t)"),
             )
 
         halves = [slice(h * HALF, (h + 1) * HALF) for h in range(2)]
@@ -309,13 +308,17 @@ def tile_picked_yenkf_half_po_kernel(tc, x_words, x_scales, w1, obs, w2, ens, of
         nc.sync.dma_start(out=out_rows[:, 3, halves[1]], in_=result[1][:, 1, halves[1]])
         for b in (2, 3):
             round_pair(nc.vector.tensor_copy, 1, block(b))
-        for b in (0, 2, 1, 3):
-            quantise_result(block(b))
-            if b >= 2:
-                nc.sync.dma_start(
-                    out=out_words.rearrange("p (h e c) -> p h e c", h=2, e=2)[:, :, b - 2, :],
-                    in_=out_codes[:].bitcast(I32).rearrange("p (h e c) -> p h e c", h=2, e=2)[:, :, b - 2, :],
-                )
+        out_codes = [
+            shared.tile([P, 2, BLOCK], U32, name="out_codes0", align_bytes=64, offset=4096 + 2 * 4 * T),
+            keep.tile([P, 2, BLOCK], U32, name="out_codes1", align_bytes=64),
+        ]
+        for e, order in enumerate(((0, 2), (3, 1))):
+            for b in order:
+                quantise_result(b)
+            nc.sync.dma_start(
+                out=out_words.rearrange("p (h e c) -> p h e c", h=2, e=2)[:, :, e, :],
+                in_=out_codes[e][:].bitcast(I32),
+            )
         for q in range(4):
             nc.sync.dma_start(
                 out=out_2[0, 4 * q : 4 * q + 4, :].bitcast(I32),

@@ -282,7 +282,8 @@ def tile_picked_yenkf_half_po_kernel(tc, x_words, x_scales, w1, obs, w2, ens, of
         nc.scalar.copy(out=update[:], in_=z_bank[0][1][:, 1, :])
         for h, cols in enumerate(halves):
             nc.vector.tensor_tensor(result[0][:, :, cols], picked[:, 0:2, cols], z_bank[h][0][:], ALU.add)
-        nc.sync.dma_start(out=out_rows[:, 0:2, :], in_=result[0][:])
+        for t in range(2):
+            nc.sync.dma_start(out=out_rows[:, t, :], in_=result[0][:, t, :])
         round_pair(nc.scalar.copy, 0, block(0))
         round_pair(nc.vector.tensor_copy, 0, block(1))
         round_pair(nc.vector.tensor_copy, 0, halves[1])
@@ -300,12 +301,11 @@ def tile_picked_yenkf_half_po_kernel(tc, x_words, x_scales, w1, obs, w2, ens, of
                 result[1][:, 1, block(b)], ens_table[3][:].indirect(block_list(b)), update[:, block(b)], ALU.add
             )
             round_pair(nc.scalar.copy, 1, block(b))
-        nc.sync.dma_start(out=out_rows[:, 3, halves[0]], in_=result[1][:, 1, halves[0]])
         for b in (2, 3):
             nc.vector.tensor_tensor(
                 result[1][:, 1, block(b)], picked_last[:, block(b - 2)], z_bank[1][1][:, 1, block(b - 2)], ALU.add
             )
-        nc.sync.dma_start(out=out_rows[:, 3, halves[1]], in_=result[1][:, 1, halves[1]])
+        nc.sync.dma_start(out=out_rows[:, 3, :], in_=result[1][:, 1, :])
         for b in (2, 3):
             round_pair(nc.vector.tensor_copy, 1, block(b))
         out_codes = [

@@ -282,8 +282,7 @@ def tile_picked_yenkf_half_po_kernel(tc, x_words, x_scales, w1, obs, w2, ens, of
         nc.scalar.copy(out=update[:], in_=z_bank[0][1][:, 1, :])
         for h, cols in enumerate(halves):
             nc.vector.tensor_tensor(result[0][:, :, cols], picked[:, 0:2, cols], z_bank[h][0][:], ALU.add)
-        for t in range(2):
-            nc.sync.dma_start(out=out_rows[:, t, :], in_=result[0][:, t, :])
+            nc.sync.dma_start(out=out_rows[:, 0:2, cols], in_=result[0][:, :, cols])
         round_pair(nc.scalar.copy, 0, block(0))
         round_pair(nc.vector.tensor_copy, 0, block(1))
         round_pair(nc.vector.tensor_copy, 0, halves[1])

@@ -213,14 +213,14 @@ def tile_picked_yenkf_half_po_kernel(tc, x_words, x_scales, w1, obs, w2, ens, of
                 in_=rr_bf[h][:, first * PACK : (first + count) * PACK],
             )
 
-        def second_product(h):
-            for t in range(PACK):
+        def second_product(h, planes, cols):
+            for t in planes:
                 nc.tensor.matmul_mx(
-                    out=z_bank[h][t // 2][:, t % 2, :],
+                    out=z_bank[h][t // 2][:, t % 2, cols],
                     lhsT=w2_codes[:, t * P : (t + 1) * P].bitcast(FP8X4),
                     lhsT_scale=w2_scale[:, t * P : (t + 1) * P],
-                    rhs=rr_codes[h][:].bitcast(FP8X4),
-                    rhs_scale=rr_scale[h][:],
+                    rhs=rr_codes[h][:, cols].bitcast(FP8X4),
+                    rhs_scale=rr_scale[h][:, cols],
                     start=True,
                     stop=True,
                 )
@@ -240,13 +240,14 @@ def tile_picked_yenkf_half_po_kernel(tc, x_words, x_scales, w1, obs, w2, ens, of
             y_bank.insert(2, bank)
         nc.vector.quantize_mx(out=w2_codes[:].bitcast(FP8X4), scales=w2_scale[:], in_=w2_bf[:])
         quantise_residual(0, 0, HALF)
-        second_product(0)
+        second_product(0, range(PACK), slice(0, HALF))
         for b in range(2):
             for e in range(2):
                 residual_dealt(b, e)
-        quantise_residual(1, 0, BLOCK)
-        quantise_residual(1, BLOCK, BLOCK)
-        second_product(1)
+        for b in range(2):
+            quantise_residual(1, b * BLOCK, BLOCK)
+            second_product(1, (0, 1), slice(b * BLOCK, (b + 1) * BLOCK))
+        second_product(1, (2, 3), slice(0, HALF))
 
         out_rows = out_0.rearrange("(p t) c -> p t c", t=PACK)
         update = shared.tile([P, HALF], F32, name="update", align_bytes=64, offset=4096)

from contextlib import ExitStack

import concourse.mybir as mybir

K, T, S, D, H, N, V = 512, 2048, 512, 8, 512, 512, 64
FLOPS = 2 * K * H * S + 2 * H * N * S

F32 = mybir.dt.float32
BF16 = mybir.dt.bfloat16
I32 = mybir.dt.int32
U32 = mybir.dt.uint32
U16 = mybir.dt.uint16
U8 = mybir.dt.uint8
FP8X4 = mybir.dt.float8_e4m3fn_x4
ALU = mybir.AluOpType

P = 128
PACK = 4
LANES = 16
BLOCK = 128
HALF = 256
BANK = 2048


def tile_picked_yenkf_half_po_kernel(tc, x_words, x_scales, w1, obs, w2, ens, offs, out_0, out_1, out_2):
    nc = tc.nc
    with ExitStack() as ctx:
        keep = ctx.enter_context(tc.tile_pool(name="keep", bufs=1))
        shared = ctx.enter_context(tc.tile_pool(name="shared", bufs=1))
        psum = ctx.enter_context(tc.psum_pool(name="psum", bufs=1))

        offsets = keep.tile([P, S // LANES], U16, name="offsets")
        x_scale_table = keep.tile([P, T], U8, name="x_scale_table", align_bytes=64)
        nc.vector.memset(x_scale_table[:, : T // 2].bitcast(I32), 0)
        nc.gpsimd.memset(x_scale_table[:, T // 2 :].bitcast(I32), 0)
        w1_rows = w1.rearrange("(p j) c -> p j c", j=PACK)
        w1_raw = [keep.tile([P, 2, H], F32, name=f"w1_raw{u}") for u in range(2)]
        nc.sync.dma_start(out=w1_raw[0][:], in_=w1_rows[:, 0:2, :])
        nc.sync.dma_start(offsets[:], offs)
        for q in range(4):
            nc.sync.dma_start(
                out=x_scale_table[32 * q : 32 * q + 4, :].bitcast(I32),
                in_=x_scales[0, 4 * q : 4 * q + 4, :].bitcast(I32),
            )
        nc.sync.dma_start(out=w1_raw[1][:], in_=w1_rows[:, 2:4, :])
        x_word_table = keep.tile([P, T], I32, name="x_word_table", align_bytes=64)
        nc.sync.dma_start(out=x_word_table[:], in_=x_words[0].rearrange("p n t -> p (n t)").bitcast(I32))
        obs_sb = keep.tile([P, PACK, V], F32, name="obs_sb")
        nc.sync.dma_start(out=obs_sb[:], in_=obs.rearrange("(p t) v -> p t v", t=PACK))
        w2_raw = keep.tile([P, PACK, N], F32, name="w2_raw")
        nc.sync.dma_start(out=w2_raw[:], in_=w2.rearrange("(p j) c -> p j c", j=PACK))
        ens_rows = ens.rearrange("(p t) c -> p t c", t=PACK)
        ens_table = []
        for t in range(PACK):
            if t in (1, 2):
                table = shared.tile([P, T], F32, name=f"ens_table{t}", align_bytes=64, offset=4096 + (t - 1) * 4 * T)
            else:
                table = keep.tile([P, T], F32, name=f"ens_table{t}")
            nc.sync.dma_start(out=table[:], in_=ens_rows[:, t, :])
            ens_table.append(table)

        def half_list(h):
            return offsets[:, h * (HALF // LANES) : (h + 1) * (HALF // LANES)]

        w1_bf = keep.tile([P, H * PACK], BF16, name="w1_bf", align_bytes=64)

        w1_dealt = w1_bf[:].rearrange("p (t m j) -> p m t j", t=PACK, j=PACK)
        nc.scalar.activation(
            out=w1_dealt[:, :, :, 0:2],
            in_=w1_raw[0][:].rearrange("p j (m t) -> p m t j", t=PACK),
            func=mybir.ActivationFunctionType.Copy,
            scale=0.5,
        )
        x_scale = keep.tile([P, S], U8, name="x_scale", align_bytes=64)
        nc.vector.tensor_copy(x_scale[:], x_scale_table[:].indirect(offsets[:]))
        x_scale_dealt = keep.tile([P, HALF], U8, name="x_scale_dealt", align_bytes=64)
        nc.vector.tensor_copy(
            x_scale_dealt[:].bitcast(I32).rearrange("p (e v) -> p e v", e=2),
            x_scale[:, HALF:].bitcast(I32).rearrange("p (v e) -> p e v", e=2),
        )
        w1_late = w1_raw[1][:].rearrange("p j (m t) -> p m t j", t=PACK)
        nc.vector.tensor_scalar(
            out=w1_dealt[:, : P // 2, :, 2:4],
            in0=w1_late[:, : P // 2],
            scalar1=0.5,
            scalar2=None,
            op0=ALU.mult,
        )
        nc.scalar.activation(
            out=w1_dealt[:, P // 2 :, :, 2:4],
            in_=w1_late[:, P // 2 :],
            func=mybir.ActivationFunctionType.Copy,
            scale=0.5,
        )
        w1_codes = keep.tile([P, H], U32, name="w1_codes", align_bytes=64)
        w1_scale = keep.tile([P, H], U8, name="w1_scale", align_bytes=64)
        nc.vector.quantize_mx(out=w1_codes[:].bitcast(FP8X4), scales=w1_scale[:], in_=w1_bf[:])

        w2_bf = shared.tile([P, N * PACK], BF16, name="w2_bf", align_bytes=64, offset=0)
        nc.scalar.copy(
            out=w2_bf[:].rearrange("p (t m j) -> p m t j", t=PACK, j=PACK),
            in_=w2_raw[:].rearrange("p j (m t) -> p m t j", t=PACK),
        )
        w2_codes = keep.tile([P, N], U32, name="w2_codes", align_bytes=64)
        w2_scale = keep.tile([P, N], U8, name="w2_scale", align_bytes=64)

        x_codes = [keep.tile([P, HALF], U32, name=f"x_codes{h}", align_bytes=64) for h in range(2)]
        nc.vector.tensor_copy(x_codes[0][:], x_word_table[:].bitcast(U32).indirect(half_list(0)))
        nc.vector.tensor_copy(
            x_codes[1][:].rearrange("p (e v d) -> p v e d", e=2, d=D // 2),
            x_word_table[:].bitcast(U32).indirect(half_list(1)),
        )
        x_scales_of = [x_scale, x_scale_dealt]

        def first_product(out, t, b, start, stop):
            cols = slice((b % 2) * BLOCK, (b % 2 + 1) * BLOCK)
            nc.tensor.matmul_mx(
                out=out[:, t, :],
                lhsT=w1_codes[:, t * P : (t + 1) * P].bitcast(FP8X4),
                lhsT_scale=w1_scale[:, t * P : (t + 1) * P],
                rhs=x_codes[b // 2][:, cols].bitcast(FP8X4),
                rhs_scale=x_scales_of[b // 2][:, cols],
                start=start,
                stop=stop,
            )

        y_bank = [psum.tile([P, PACK, BLOCK], F32, name=f"y_bank{b}", offset=b * BANK) for b in range(2)]
        pair_bank = psum.tile([P, PACK, BLOCK], F32, name="pair_bank", offset=2 * BANK)
        for b in (0, 1):
            for t in range(PACK):
                first_product(y_bank[b], t, b, True, True)
        for t in range(PACK):
            first_product(pair_bank, t, 2, True, False)
            first_product(pair_bank, t, 3, False, True)

        groups = BLOCK // D
        sums = [keep.tile([P, 2 * groups, PACK], F32, name=f"sums{h}") for h in range(2)]
        om = [keep.tile([P, 2 * groups, PACK], F32, name=f"om{h}") for h in range(2)]
        rr_bf = [
            keep.tile([P, HALF * PACK], BF16, name="rr_bf0", align_bytes=64),
            shared.tile([P, HALF * PACK], BF16, name="rr_bf1", align_bytes=64, offset=0),
        ]
        rr_codes = [
            shared.tile([P, HALF], U32, name="rr_codes0", align_bytes=64, offset=2048),
            keep.tile([P, HALF], U32, name="rr_codes1", align_bytes=64),
        ]
        rr_scale = [keep.tile([P, HALF], U8, name=f"rr_scale{h}", align_bytes=64) for h in range(2)]
        picked = keep.tile([P, PACK - 1, S], F32, name="picked")
        for t in range(PACK - 1):
            nc.scalar.activation(
                out=picked[:, t, :],
                in_=ens_table[t][:].indirect(offsets[:]),
                func=mybir.ActivationFunctionType.Copy,
            )
        result = [
            keep.tile([P, 2, S], F32, name="result0"),
            keep.tile([P, 2, S], F32, name="result1"),
        ]

        z_bank = [
            [psum.tile([P, 2, HALF], F32, name=f"z_bank{h}{u}", offset=(2 * h + u + 3) * BANK) for u in range(2)]
            for h in range(2)
        ]

        def member_sums(b):
            nc.vector.tensor_reduce(
                out=sums[b // 2][:, (b % 2) * groups : (b % 2 + 1) * groups, :],
                in_=y_bank[b][:].rearrange("p t (v d) -> p v t d", d=D),
                axis=mybir.AxisListType.X,
                op=ALU.add,
            )

        def member_sums_of_pairs():
            nc.vector.tensor_reduce(
                out=sums[1][:],
                in_=pair_bank[:].rearrange("p t (v d) -> p v t d", d=D // 2),
                axis=mybir.AxisListType.X,
                op=ALU.add,
            )

        def residual_dealt(b, e):
            span = slice(b * groups, (b + 1) * groups)
            nc.vector.tensor_tensor(
                out=rr_bf[1][:].rearrange("p (v e d t) -> p v e d t", e=2, d=D // 2, t=PACK)[:, span, e],
                in0=om[1][:, span, :].unsqueeze(2).broadcast_to([P, groups, D // 2, PACK]),
                in1=y_bank[2 + e][:].rearrange("p t (v d) -> p v d t", d=D // 2)[:, span],
                op=ALU.subtract,
            )

        def innovation(h, first, count):
            nc.vector.scalar_tensor_tensor(
                out=om[h][:, first : first + count, :],
                in0=sums[h][:, first : first + count, :],
                scalar=-1.0 / D,
                in1=obs_sb[:, :, 2 * h * groups + first : 2 * h * groups + first + count].rearrange("p t v -> p v t"),
                op0=ALU.mult,
                op1=ALU.add,
            )

        def residual(b):
            span = slice((b % 2) * BLOCK * PACK, (b % 2 + 1) * BLOCK * PACK)
            nc.vector.tensor_tensor(
                out=rr_bf[b // 2][:, span].rearrange("p (v d t) -> p v d t", d=D, t=PACK),
                in0=om[b // 2][:, (b % 2) * groups : (b % 2 + 1) * groups, :].unsqueeze(2).broadcast_to([P, groups, D, PACK]),
                in1=y_bank[b][:].rearrange("p t (v d) -> p v d t", d=D),
                op=ALU.subtract,
            )

        def quantise_residual(h, first, count):
            nc.vector.quantize_mx(
                out=rr_codes[h][:, first : first + count].bitcast(FP8X4),
                scales=rr_scale[h][:, first : first + count],
                in_=rr_bf[h][:, first * PACK : (first + count) * PACK],
            )

        def second_product(h, planes, cols):
            for t in planes:
                nc.tensor.matmul_mx(
                    out=z_bank[h][t // 2][:, t % 2, cols],
                    lhsT=w2_codes[:, t * P : (t + 1) * P].bitcast(FP8X4),
                    lhsT_scale=w2_scale[:, t * P : (t + 1) * P],
                    rhs=rr_codes[h][:, cols].bitcast(FP8X4),
                    rhs_scale=rr_scale[h][:, cols],
                    start=True,
                    stop=True,
                )

        member_sums(0)
        member_sums(1)
        innovation(0, 0, groups)
        innovation(0, groups, groups)
        residual(0)
        member_sums_of_pairs()
        residual(1)
        innovation(1, 0, 2 * groups)
        for b in (3, 2):
            bank = psum.tile([P, PACK, BLOCK], F32, name=f"y_bank{b}", offset=(b - 1) * BANK)
            for t in range(PACK):
                first_product(bank, t, b, True, True)
            y_bank.insert(2, bank)
        nc.vector.quantize_mx(out=w2_codes[:].bitcast(FP8X4), scales=w2_scale[:], in_=w2_bf[:])
        quantise_residual(0, 0, HALF)
        second_product(0, range(PACK), slice(0, HALF))
        for b in range(2):
            for e in range(2):
                residual_dealt(b, e)
        for b in range(2):
            quantise_residual(1, b * BLOCK, BLOCK)
            second_product(1, (0, 1), slice(b * BLOCK, (b + 1) * BLOCK))
        second_product(1, (2, 3), slice(0, HALF))

        out_rows = out_0.rearrange("(p t) c -> p t c", t=PACK)
        update = shared.tile([P, HALF], F32, name="update", align_bytes=64, offset=4096)
        picked_last = shared.tile([P, HALF], F32, name="picked_last", align_bytes=64, offset=4096 + 2 * 4 * T)
        out_bf_first = shared.tile([P, BLOCK, PACK], BF16, name="out_bf_first", align_bytes=64, offset=4096 + 4 * T)
        out_bf_rest = keep.tile([P, S - BLOCK, PACK], BF16, name="out_bf_rest", align_bytes=64)

        def staged(cols):
            if cols.start < BLOCK:
                return out_bf_first[:, cols, :]
            return out_bf_rest[:, cols.start - BLOCK : cols.stop - BLOCK, :]

        out_scale = keep.tile([P, S], U8, name="out_scale", align_bytes=64)
        out_words = out_1[0].rearrange("p n t -> p (n t)").bitcast(I32)

        def block(b):
            return slice(b * BLOCK, (b + 1) * BLOCK)

        def block_list(b):
            return offsets[:, b * (BLOCK // LANES) : (b + 1) * (BLOCK // LANES)]

        def round_pair(copy, u, cols):
            copy(out=staged(cols)[:, :, 2 * u : 2 * u + 2], in_=result[u][:, :, cols].rearrange("p e c -> p c e"))

        def quantise_result(b):
            nc.vector.quantize_mx(
                out=out_codes[b % 2][:, b // 2, :].bitcast(FP8X4),
                scales=out_scale[:, block(b)],
                in_=staged(block(b)).rearrange("p c t -> p (c t)"),
            )

        halves = [slice(h * HALF, (h + 1) * HALF) for h in range(2)]
        nc.scalar.copy(out=update[:], in_=z_bank[0][1][:, 1, :])
        for h, cols in enumerate(halves):
            nc.vector.tensor_tensor(result[0][:, :, cols], picked[:, 0:2, cols], z_bank[h][0][:], ALU.add)
            nc.sync.dma_start(out=out_rows[:, 0:2, cols], in_=result[0][:, :, cols])
        round_pair(nc.scalar.copy, 0, block(0))
        round_pair(nc.vector.tensor_copy, 0, block(1))
        round_pair(nc.vector.tensor_copy, 0, halves[1])
        for h, cols in enumerate(halves):
            nc.vector.tensor_tensor(result[1][:, 0, cols], picked[:, 2, cols], z_bank[h][1][:, 0, :], ALU.add)
        nc.sync.dma_start(out=out_rows[:, 2, :], in_=result[1][:, 0, :])
        for b in (2, 3):
            nc.scalar.activation(
                out=picked_last[:, block(b - 2)],
                in_=ens_table[3][:].indirect(block_list(b)),
                func=mybir.ActivationFunctionType.Copy,
            )
        for b in (0, 1):
            nc.vector.tensor_tensor(
                result[1][:, 1, block(b)], ens_table[3][:].indirect(block_list(b)), update[:, block(b)], ALU.add
            )
            round_pair(nc.scalar.copy, 1, block(b))
        for b in (2, 3):
            nc.vector.tensor_tensor(
                result[1][:, 1, block(b)], picked_last[:, block(b - 2)], z_bank[1][1][:, 1, block(b - 2)], ALU.add
            )
        nc.sync.dma_start(out=out_rows[:, 3, :], in_=result[1][:, 1, :])
        for b in (2, 3):
            round_pair(nc.vector.tensor_copy, 1, block(b))
        out_codes = [
            shared.tile([P, 2, BLOCK], U32, name="out_codes0", align_bytes=64, offset=4096 + 2 * 4 * T),
            keep.tile([P, 2, BLOCK], U32, name="out_codes1", align_bytes=64),
        ]
        for e, order in enumerate(((0, 2), (3, 1))):
            for b in order:
                quantise_result(b)
            nc.sync.dma_start(
                out=out_words.rearrange("p (h e c) -> p h e c", h=2, e=2)[:, :, e, :],
                in_=out_codes[e][:].bitcast(I32),
            )
        for q in range(4):
            nc.sync.dma_start(
                out=out_2[0, 4 * q : 4 * q + 4, :].bitcast(I32),
                in_=out_scale[32 * q : 32 * q + 4, :].bitcast(I32),
            )
